import numpy as np
import ml_dtypes


def mxq(x, axis, fmt="e4m3"):
    dtype, down = {"e4m3": (ml_dtypes.float8_e4m3fn, 7), "e5m2": (ml_dtypes.float8_e5m2, 14)}[fmt]
    v = np.moveaxis(np.asarray(x, np.float32).astype(ml_dtypes.bfloat16).astype(np.float64), axis, -1)
    blocks = v.reshape(v.shape[:-1] + (-1, 32))
    amax = np.abs(blocks).max(-1, keepdims=True)
    byte = np.maximum(np.where(amax > 0, np.frexp(amax)[1] - 1 + 127, 0) - down, 1)
    scale = np.exp2(byte - 127.0)
    codes = (blocks / scale).astype(np.float32).astype(dtype).astype(np.float64)
    return np.moveaxis((codes * scale).reshape(v.shape), -1, axis)


WIDE = False


def mx_kscale(k):
    if not WIDE:
        return np.ones(k)
    levels = np.array([10, -10, 5, -5, 0])
    if k % 512:
        return np.exp2(np.random.permutation(np.resize(levels, k // 32))).repeat(32)
    a = np.empty((k // 512, 16))
    for p in range(k // 512):
        a[p, :8] = np.random.permutation(np.resize(levels, 8))
        for g in range(8):
            far = levels[np.abs(levels - a[p, g]) >= 10]
            a[p, g + 8] = far[np.random.randint(len(far))]
    return np.exp2(a.ravel()).repeat(32)


BF16 = ml_dtypes.bfloat16


def bf(x):
    return np.asarray(x, np.float32).astype(BF16)


def f64(x):
    return np.asarray(x).astype(np.float64)


E2M1 = np.array([0.0, 0.5, 1.0, 1.5, 2.0, 3.0, 4.0, 6.0, -0.0, -0.5, -1.0, -1.5, -2.0, -3.0, -4.0, -6.0])


def pack_weight(w, fmt):
    k, n = w.shape
    w = f64(bf(w)).reshape(k // 32, 32, n)
    amax = np.abs(w).max(1)
    if fmt == "e4m3":
        byte = np.frexp(amax)[1] - 1 + 127 - 7
    else:
        mant, ex = np.frexp(amax / 6.0)
        byte = np.where(mant > 0.5, ex, ex - 1) + 127
    byte = np.clip(np.where(amax > 0, byte, 1), 1, 254)
    scaled = (w * np.exp2(127.0 - byte)[:, None, :]).reshape(k, n).astype(np.float32)
    by_word = np.ascontiguousarray(scaled.reshape(k // 512, 128, 4, n).transpose(0, 1, 3, 2))
    if fmt == "e4m3":
        words = by_word.astype(ml_dtypes.float8_e4m3fn).view(np.uint8)
    else:
        c = by_word.astype(ml_dtypes.float4_e2m1fn).view(np.uint8) & 0xF
        words = c[..., 0::2] | (c[..., 1::2] << 4)
    return np.ascontiguousarray(words), np.ascontiguousarray(byte.astype(np.uint8).reshape(k // 512, 16, n))


def unpack_weight(words, scales, fmt):
    g, p, n, _ = words.shape
    if fmt == "e4m3":
        vals = np.ascontiguousarray(words).view(ml_dtypes.float8_e4m3fn).astype(np.float64)
    else:
        nib = np.empty((g, p, n, 4), np.uint8)
        nib[..., 0::2] = words & 0xF
        nib[..., 1::2] = words >> 4
        vals = E2M1[nib]
    vals = vals * np.repeat(np.exp2(scales.astype(np.float64) - 127.0), 8, axis=1)[..., None]
    return vals.transpose(0, 1, 3, 2).reshape(g * 512, n)
def pack4(w):
    words, scales = pack_weight(w, "e2m1")
    return words.reshape(words.shape[0], 128, -1), scales


def unpack4(words, scales):
    return unpack_weight(words.reshape(words.shape[0], 128, -1, 2), scales, "e2m1")


def planes(Y):
    n, m = Y.shape
    b = f64(bf(Y)).reshape(n // 32, 32, m)
    amax = np.abs(b).max(1)
    byte = np.clip(np.where(amax > 0, np.frexp(amax)[1] - 1 + 127 - 7, 1), 1, 254)
    codes = (b * np.exp2(127.0 - byte)[:, None, :]).reshape(n, m).astype(np.float32).astype(ml_dtypes.float8_e4m3fn).view(np.uint8)
    words = codes.reshape(n // 512, 128, 4, m).transpose(0, 1, 3, 2)
    return np.ascontiguousarray(words), np.ascontiguousarray(byte.astype(np.uint8).reshape(n // 512, 16, m))


B, I, J, P, Q = 4, 512, 512, 512, 512


def silu(v):
    return v / (1.0 + np.exp(-v))


def two_sided(xq, a, b):
    t = xq @ b
    return a @ mxq(t, 1, "e4m3")


def setup_inputs():
    s, u = mx_kscale(J), mx_kscale(I)
    x = np.random.standard_normal((B, I, J)) * s[None, None, :] * u[None, :, None]
    b1 = np.random.standard_normal((J, Q)) / np.sqrt(J) / s[:, None]
    b2 = np.random.standard_normal((J, Q)) / np.sqrt(J) / s[:, None]
    a1 = np.random.standard_normal((P, I)) / np.sqrt(I) / u[None, :]
    a2 = np.random.standard_normal((P, I)) / np.sqrt(I) / u[None, :]
    c = 0.5 * np.random.standard_normal((P, Q))
    b1_words, b1_scales = pack4(b1)
    b2_words, b2_scales = pack4(b2)
    a1_words, a1_scales = pack4(a1.T)
    a2_words, a2_scales = pack4(a2.T)
    return {"x": bf(x), "b1_words": b1_words, "b1_scales": b1_scales, "b2_words": b2_words, "b2_scales": b2_scales,
            "a1_words": a1_words, "a1_scales": a1_scales, "a2_words": a2_words, "a2_scales": a2_scales, "c": bf(c)}


def core(x, b1_words, b1_scales, b2_words, b2_scales, a1_words, a1_scales, a2_words, a2_scales, c):
    xq = mxq(f64(x), 2, "e4m3")
    u1 = two_sided(xq, unpack4(a1_words, a1_scales).T, unpack4(b1_words, b1_scales))
    u2 = two_sided(xq, unpack4(a2_words, a2_scales).T, unpack4(b2_words, b2_scales))
    z = u1 + u2 + f64(c)[None, :, :]
    return silu(z)


def reference(x, b1_words, b1_scales, b2_words, b2_scales, a1_words, a1_scales, a2_words, a2_scales, c):
    R_out = core(x, b1_words, b1_scales, b2_words, b2_scales, a1_words, a1_scales, a2_words, a2_scales, c)
    words, scales = planes(np.moveaxis(R_out, 2, 0).reshape(512, -1))
    return R_out, words, scales

from contextlib import ExitStack

import concourse.mybir as mybir
from concourse.masks import make_identity

F32 = mybir.dt.float32
BF16 = mybir.dt.bfloat16
I32 = mybir.dt.int32
U32 = mybir.dt.uint32
U8 = mybir.dt.uint8
FP8X4 = mybir.dt.float8_e4m3fn_x4
FP4X4 = mybir.dt.float4_e2m1fn_x4
SILU = mybir.ActivationFunctionType.Silu
ADD = mybir.AluOpType.add

B, D = 4, 512
P = 128
FLOPS = 2 * 2 * 2 * B * D * D * D

STEPS = ["XX...XXTTTTTTTT", "TTXXTZTZTTTToZZa", "TTXXTZTZTTTToZZa", "TTXXTZTZTTTToZZa", "..ZZZ.Z.o.....a.b"]
D_XC, D_XQ, D_TC, D_TQ, D_ZA, D_ZS, D_ZC, D_OC, D_OQ = 3, 2, 2, 3, 2, 3, 2, 3, 4
T_ON_VECTOR = ((0, 4), (0, 4), (0, 4), (0, 5))


def tile_ranktwokroneckersumlayer_x2_kernel(
    tc, x, b1_words, b1_scales, b2_words, b2_scales, a1_words, a1_scales, a2_words, a2_scales, c, out_0, out_1, out_2
):
    nc = tc.nc
    with ExitStack() as ctx:
        keep = ctx.enter_context(tc.tile_pool(name="keep", bufs=1))
        work = ctx.enter_context(tc.tile_pool(name="work", bufs=4))
        psum = ctx.enter_context(tc.psum_pool(name="psum", bufs=2))
        ctx.enter_context(tc.manual_schedule())

        w_scales = keep.tile([P, 4, D], U8, name="w_scales", align_bytes=256)
        nc.vector.memset(w_scales[:].rearrange("p w n -> p (w n)").bitcast(I32), 0)
        warm = keep.tile([P, 1], F32, name="warm")
        nc.vector.memset(warm[:], 0.0)
        ident = keep.tile([P, P], F32, name="ident")
        make_identity(nc, ident[:])
        warm_out = keep.tile([P, 1], F32, name="warm_out")
        nc.scalar.activation(warm_out[:], warm[:], SILU)

        x_in = [keep.tile([P, 4, D], BF16, name=f"x_in{n}") for n in range(B)]

        def load_x(n, b):
            rows = x[n].rearrange("(m t) j -> m t j", t=4)
            nc.sync.dma_start(out=x_in[n][:, 2 * b : 2 * b + 2, :], in_=rows[:, 2 * b : 2 * b + 2, :])

        w_words = [keep.tile([P, 2 * D], U8, name=f"w_words{w}", align_bytes=256) for w in range(4)]
        words_in = [b1_words, b2_words, a1_words, a2_words]
        scales_in = [b1_scales, b2_scales, a1_scales, a2_scales]

        def load_words(w):
            nc.sync.dma_start(out=w_words[w][:].bitcast(I32), in_=words_in[w][0].bitcast(I32))

        def load_scales(w):
            queue = nc.scalar if w < 2 else nc.gpsimd
            for q in range(4):
                queue.dma_start(
                    out=w_scales[32 * q : 32 * q + 4, w, :].bitcast(I32),
                    in_=scales_in[w][0, 4 * q : 4 * q + 4, :].bitcast(I32),
                )

        c_sb = keep.tile([P, 4, D], BF16, name="c_sb")
        load_x(0, 0)
        load_x(0, 1)
        load_scales(0)
        load_words(0)
        load_words(1)
        load_scales(1)
        load_scales(2)
        load_scales(3)
        load_x(1, 0)
        load_x(1, 1)
        load_words(2)
        load_words(3)
        nc.sync.dma_start(out=c_sb[:], in_=c.rearrange("(j p) q -> p j q", p=P))
        for n in range(2, B):
            load_x(n, 0)
            load_x(n, 1)

        x_codes = [keep.tile([P, D], U32, name=f"x_codes{n}", align_bytes=256) for n in range(B)]
        x_scales = [keep.tile([P, D], U8, name=f"x_scales{n}", align_bytes=256) for n in range(B)]
        t_codes = [[keep.tile([P, D], U32, name=f"t_codes{n}{s}", align_bytes=256) for s in range(2)] for n in range(B)]
        t_scales = [[keep.tile([P, D], U8, name=f"t_scales{n}{s}", align_bytes=256) for s in range(2)] for n in range(B)]
        o_codes = keep.tile([P, B * D], I32, name="o_codes", align_bytes=256)
        o_scales = keep.tile([P, B * D], U8, name="o_scales", align_bytes=256)

        o_bf = {}

        def copy(on_vector, out, in_):
            if on_vector:
                nc.vector.tensor_copy(out=out, in_=in_)
            else:
                nc.scalar.copy(out=out, in_=in_)

        steps = []
        for n in range(B + 1):
            count = {"X": 0, "T": 0, "Z": 0}
            for ch in STEPS[n]:
                k = count.get(ch, 0)
                if ch == "X":
                    m = 0 if (n == 0 and k < 2) else n + 1
                    if m < B:
                        steps.append(("X", m, k % 2))
                elif ch == "T":
                    steps.append(("T", n, k))
                elif ch == "Z":
                    steps.append(("Z", n - 1, k))
                elif ch == "o":
                    if n >= 2:
                        steps.append(("O", n - 2, 1))
                elif ch == "a":
                    steps.append(("O", n - 1, 0))
                elif ch == "b":
                    steps.append(("O", n - 1, 1))
                else:
                    steps.append((".", 0, 0))
                count[ch] = k + 1
        waiting = [[] for i in range(len(steps) + 24)]

        def later(i, delay, fn):
            waiting[i + delay].append(fn)

        def step_x(i, n, b):
            bank = psum.tile([P, 2, 2, P], F32, name="bank_x", tag="tr", bufs=2)
            for s in range(2):
                row_words = x_in[n][:, 2 * b + s, :].bitcast(F32)
                for u in range(2):
                    nc.tensor.transpose(bank[:, s, u, :], row_words[:, u::2], ident[:])

            def do_copy(i):
                grouped = work.tile([P, 1024], BF16, name="x_grouped", tag="x_grouped", bufs=4, align_bytes=256)
                copy(
                    b == 1,
                    grouped[:].bitcast(F32).rearrange("p (s m u) -> p s m u", s=2, u=2),
                    bank[:].rearrange("p s u m -> p s m u"),
                )

                def quant(i):
                    cols = slice(256 * b, 256 * b + 256)
                    nc.vector.quantize_mx(out=x_codes[n][:, cols].bitcast(FP8X4), scales=x_scales[n][:, cols], in_=grouped[:])

                later(i, D_XQ, quant)

            later(i, D_XC, do_copy)

        grouped_t = {}

        def step_t(i, n, k):
            s, h = k // 4, k % 4
            bank = psum.tile([P, 4, P], F32, name="bank_t", tag="t", bufs=4)
            for t in range(4):
                cols = slice(P * t, P * t + P)
                nc.tensor.matmul_mx(
                    out=bank[:, t, :],
                    lhsT=x_codes[n][:, cols].bitcast(FP8X4),
                    lhsT_scale=x_scales[n][:, cols],
                    rhs=w_words[s][:, 256 * h : 256 * h + 256].bitcast(FP4X4),
                    rhs_scale=w_scales[:, s, P * h : P * h + P],
                    start=True,
                    stop=True,
                )

            def do_copy(i):
                if h == 0:
                    grouped_t[0] = work.tile([P, 4 * D], BF16, name="t_grouped", tag="t_grouped", bufs=4, align_bytes=256)
                grouped = grouped_t[0]
                part = slice(512 * h, 512 * h + 512)
                copy(k in T_ON_VECTOR[n], grouped[:, part].rearrange("p (q t) -> p q t", t=4), bank[:].rearrange("p t q -> p q t"))

                def quant(i):
                    nc.vector.quantize_mx(out=t_codes[n][s][:].bitcast(FP8X4), scales=t_scales[n][s][:], in_=grouped[:])

                if h == 3:
                    later(i, D_TQ, quant)

            later(i, D_TC, do_copy)

        def step_z(i, n, j):
            bank = psum.tile([P, D], F32, name="bank_z", tag="z", bufs=2)
            for s in range(2):
                nc.tensor.matmul_mx(
                    out=bank[:],
                    lhsT=w_words[2 + s][:, 256 * j : 256 * j + 256].bitcast(FP4X4),
                    lhsT_scale=w_scales[:, 2 + s, P * j : P * j + P],
                    rhs=t_codes[n][s][:].bitcast(FP8X4),
                    rhs_scale=t_scales[n][s][:],
                    start=(s == 0),
                    stop=(s == 1),
                )

            def do_add(i):
                v = work.tile([P, D], F32, name="v", tag="v", bufs=4)
                nc.vector.tensor_tensor(out=v[:], in0=bank[:], in1=c_sb[:, j, :], op=ADD)

                def do_silu(i):
                    o = work.tile([P, D], F32, name="o", tag="o", bufs=6)
                    nc.scalar.activation(o[:], v[:], SILU)
                    nc.sync.dma_start(out=out_0[n, P * j : P * j + P, :], in_=o[:])

                    def do_cast(i):
                        ob = work.tile([P, D], BF16, name="ob", tag="ob", bufs=6)
                        nc.vector.tensor_copy(
                            out=ob[:].rearrange("p (u k e) -> p u k e", u=2, e=2),
                            in_=o[:].rearrange("p (k u e) -> p u k e", u=2, e=2),
                        )
                        o_bf[(n, j)] = ob

                    later(i, D_ZC, do_cast)

                later(i, D_ZS, do_silu)

            later(i, D_ZA, do_add)

        def step_o(i, n, b):
            bank = psum.tile([P, 2, 2, P], F32, name="bank_o", tag="tr", bufs=2)
            for s in range(2):
                ob_words = o_bf[(n, 2 * b + s)][:].bitcast(F32)
                for u in range(2):
                    nc.tensor.transpose(bank[:, s, u, :], ob_words[:, P * u : P * u + P], ident[:])

            def do_copy(i):
                grouped = work.tile([P, 1024], BF16, name="o_grouped", tag="o_grouped", bufs=4, align_bytes=256)
                copy(
                    False,
                    grouped[:].bitcast(F32).rearrange("p (s m u) -> p s m u", s=2, u=2),
                    bank[:].rearrange("p s u m -> p s m u"),
                )

                def quant(i):
                    c0 = D * n + 256 * b
                    cols = slice(c0, c0 + 256)
                    nc.vector.quantize_mx(out=o_codes[:, cols].bitcast(FP8X4), scales=o_scales[:, cols], in_=grouped[:])
                    nc.sync.dma_start(
                        out=out_1[0, :, cols, :].rearrange("p m t -> p (m t)").bitcast(I32), in_=o_codes[:, cols]
                    )
                    if b == 1 and n >= B - 2:
                        s_cols = slice(0, 1536) if n == B - 2 else slice(1536, 2048)
                        for q in range(4):
                            nc.sync.dma_start(
                                out=out_2[0, 4 * q : 4 * q + 4, s_cols].bitcast(I32),
                                in_=o_scales[32 * q : 32 * q + 4, s_cols].bitcast(I32),
                            )

                later(i, D_OQ, quant)

            later(i, D_OC, do_copy)

        emit = {"X": step_x, "T": step_t, "Z": step_z, "O": step_o}
        for i in range(len(waiting)):
            for fn in waiting[i]:
                fn(i)
            if i < len(steps) and steps[i][0] != ".":
                kind, n, k = steps[i]
                emit[kind](i, n, k)
